import numpy as np, ml_dtypes
CORES = [16,18,20,22]
N = 4
BF = ml_dtypes.bfloat16
def gentries(a):
    return np.ascontiguousarray(a.reshape(8, 16, -1).transpose(0, 2, 1)).reshape(8, -1)
def gtable(e):
    e = np.asarray(e); return np.ascontiguousarray(e.reshape(8, -1, 16).transpose(0, 2, 1)).reshape(128, -1).astype(np.int32)
P, S, H, C, D, TH = 2048, 256, 4096, 4, 3, 11008
W = P + (N - 1) * S
def stored(v):
    return np.stack([gtable(np.reshape(v[r], (8, -1))) for r in range(N)])
def setup_inputs(rng):
    v = rng.integers(0, 8, (N, 8, 16, P)) + rng.integers(32, 128, (N, 8, 1, P)) * (np.arange(16)[:, None] == rng.integers(0, 16, (N, 8, 1, P)))
    return {"x": v.reshape(N, 128, P).astype(np.float32).astype(BF), "sus": np.floor(256 * rng.random((N, 128, H)) ** 2).astype(np.float32).astype(BF),
            "hist": stored(rng.integers(0, H, (N, 8, P))), "home": stored(rng.integers(0, W, (N, 8, C, P))), "away": stored(rng.integers(0, W, (N, 8, C, P))),
            "shown": stored(rng.integers(0, P, (N, 8, N - 1, S)))}
def setup_inputs_ties(rng):
    d = setup_inputs(rng); b = TH // 64
    d["x"] = (64 * (rng.random((N, 128, P)) * C < 0.25)).astype(np.float32).astype(BF)
    d["sus"] = rng.choice(np.array([0, 0, b, b + 1]), (N, 128, H)).astype(np.float32).astype(BF); return d
def setup_inputs_ends(rng):
    d = setup_inputs(rng); e = np.array([0, P - 1] + [P + k * S for k in range(N - 1)] + [P + k * S + S - 1 for k in range(N - 1)])
    for a, w in (("home", e), ("away", e), ("shown", e[:2]), ("hist", np.array([0, 15, H - 16, H - 1]))):
        d[a] = np.where(rng.random(d[a].shape) < 0.5, rng.choice(w, d[a].shape), d[a]).astype(np.int32)
    return d
def setup_inputs_one(rng):
    d = setup_inputs(rng); o = np.ones((1, 1, P), np.int64)
    d["hist"] = stored(rng.integers(0, H, (N, 8, 1)) * o); d["home"] = stored(rng.integers(0, W, (N, 8, 1)) * np.ones((1, 1, C * P), np.int64)); return d
def setup_inputs_far(rng):
    d = setup_inputs(rng); own = rng.integers(0, P, (N, 8, C, P)); out = rng.integers(P, W, (N, 8, C, P)); even = (np.arange(N) % 2 == 0)[:, None, None, None]
    d["home"] = stored(np.where(even, out, own)); d["away"] = stored(np.where(even, own, out)); return d
def setup_inputs_spread(rng):
    d = setup_inputs(rng); s = np.where(rng.random((N, 8, 1, P)) < 0.5, rng.integers(0, 4, (N, 8, 1, P)), rng.integers(0, 9, (N, 8, 1, P)))
    d["x"] = np.floor(256 * rng.random((N, 8, 16, P)) * np.exp2(-s)).reshape(N, 128, P).astype(np.float32).astype(BF)
    d["sus"] = np.floor(256 * rng.random((N, 8, 16, H)) * np.exp2(-rng.integers(0, 6, (N, 8, 1, H)))).reshape(N, 128, H).astype(np.float32).astype(BF)
    for a, n, k in (("hist", H, P), ("home", W, C * P), ("away", W, C * P), ("shown", P, (N - 1) * S)):
        d[a] = stored((np.floor(n * rng.random((N, 8, k)) ** 3).astype(np.int64) + rng.integers(0, n, (N, 8, 1))) % n)
    return d
def check_inputs(d):
    bad = []
    for a in ("x", "sus"):
        v = d[a].astype(np.float32)
        if not ((v >= 0) & (v <= 255) & (v == np.floor(v))).all(): bad.append(a)
    for a, n in (("hist", H), ("home", W), ("away", W), ("shown", P)):
        if not ((d[a] >= 0) & (d[a] < n)).all(): bad.append(a)
    return bad
def reference(x, sus, hist, home, away, shown):
    load = x.astype(np.float32).astype(np.int64).reshape(N, 8, 16, P); tab = sus.astype(np.float32).astype(np.int64).reshape(N, 8, 16, H)
    code = np.stack([gentries(hist[r]) for r in range(N)]).astype(np.int64); ill = np.zeros((N, 8, P), bool)
    near = np.stack([gentries(home[r]) for r in range(N)]).reshape(N, 8, C, P); far = np.stack([gentries(away[r]) for r in range(N)]).reshape(N, 8, C, P)
    give = np.stack([gentries(shown[r]) for r in range(N)]).reshape(N, 8, N - 1, S)
    for day in range(D):
        new = load >> 1
        for r in range(N):
            parts = [load[r]]
            for q in range(N):
                if q != r: parts.append(np.take_along_axis(load[q], give[q][:, None, r if r < q else r - 1], 2))
            win = np.concatenate(parts, 2)
            con = np.where(ill[r][:, None], far[r], near[r]).reshape(8, 1, C * P)
            pressure = np.sum(np.take_along_axis(win, con, 2).reshape(8, 16, C, P), axis=2)
            score = pressure * np.take_along_axis(tab[r], code[r][:, None], 2)
            best = np.argmax(score, axis=1); hit = np.max(score, axis=1) > TH
            new[r] += 64 * ((np.arange(16)[:, None] == best[:, None]) & hit[:, None])
            code[r] = np.where(hit, (16 * code[r] + best) & (H - 1), code[r]); ill[r] = hit
        load = new
    return {"y": load.reshape(N, 128, P).astype(np.float32), "h": stored(code).astype(np.float32)}

from concourse.bass import DstId, RemoteDMATransfer
from concourse.mybir import AluOpType, ActivationFunctionType

P, S, W, H, TH, DAYS = 2048, 256, 2816, 4096, 11008, 3
N, U = 512, 4
GROUPS = [(0, 2), (2, 3), (3, 4)]
BATCHES = [(0, 4)]
PAIRED = {(3, 0), (3, 1), (3, 2), (3, 3)}
TWO = ["xx", "uu"]

SCRATCH = {
    "win1": ("sbuf", [128, W], "bfloat16"), "win2": ("sbuf", [128, W], "bfloat16"), "win3": ("sbuf", [128, W], "bfloat16"),
    "tab": ("sbuf", [128, H], "bfloat16"),
    "shown_i": ("sbuf", [128, 48], "int32"), "shown_u": ("sbuf", [128, 48], "uint16"),
    "c1": ("sbuf", [128, 128], "int32"), "c2": ("sbuf", [128, 128], "int32"), "c3": ("sbuf", [128, 128], "int32"),
    "c4": ("sbuf", [128, 128], "float32"),
    "hu1": ("sbuf", [128, 128], "uint16"), "hu2": ("sbuf", [128, 128], "uint16"), "hu3": ("sbuf", [128, 128], "uint16"),
    "home_i": ("sbuf", [128, 512], "int32"), "away_i": ("sbuf", [128, 512], "int32"), "dif": ("sbuf", [128, 512], "float32"),
    "cu1": ("sbuf", [128, 512], "uint16"), "cu2": ("sbuf", [128, 512], "uint16"), "cu3": ("sbuf", [128, 512], "uint16"),
    "lowc": ("sbuf", [128, 128], "int32"), "lowx": ("sbuf", [128, 128], "float32"), "ac": ("sbuf", [128, 128], "float32"),
    "t1": ("sbuf", [128, 128], "float32"), "t2": ("sbuf", [128, 128], "float32"),
    "hd": ("sbuf", [128, 512], "float32"), "mg": ("sbuf", [128, 512], "float32"),
    "gc": ("sbuf", [128, 4 * P], "bfloat16"), "gs": ("sbuf", [128, P], "bfloat16"),
    "g0": ("sbuf", [128, P], "float32"), "g2": ("sbuf", [128, P], "float16"),
    "st0": ("sbuf", [128, P], "bfloat16"), "st1": ("sbuf", [128, P], "bfloat16"),
    "sc": ("sbuf", [128, P], "float32"), "fs": ("sbuf", [128, P], "float32"),
    "zi": ("sbuf", [128, 32 * U], "int32"), "zz": ("sbuf", [128, 32 * U], "int32"),
    "feat": ("sbuf", [128, 96 * U], "bfloat16"), "tts": ("sbuf", [128, 128 * U], "bfloat16"),
    "h1": ("sbuf", [128, P], "bfloat16"), "h2": ("sbuf", [128, P], "bfloat16"), "h3": ("sbuf", [128, P], "bfloat16"),
    "hr": ("sbuf", [128, P], "bfloat16"),
    "snd1": ("sbuf", [128, 3 * S], "bfloat16"), "snd2": ("sbuf", [128, 3 * S], "bfloat16"), "snd3": ("sbuf", [128, 3 * S], "bfloat16"),
    "yo": ("sbuf", [128, P], "float32"),
    "ones": ("sbuf", [128, 128], "bfloat16"), "neg32": ("sbuf", [128, 128], "bfloat16"),
    "ri": ("sbuf", [128, 128], "bfloat16"), "rih": ("sbuf", [128, 128], "float16"),
    "ris": ("sbuf", [128, 128], "bfloat16"), "idn": ("sbuf", [128, 128], "bfloat16"),
    "ev": ("sbuf", [128, 512], "bfloat16"), "em": ("sbuf", [128, 512], "bfloat16"),
    "mz": ("sbuf", [128, 128], "bfloat16"), "lm": ("sbuf", [128, 512], "bfloat16"),
    "s1f": ("sbuf", [128, 16], "float32"), "s1q": ("sbuf", [128, 16], "float32"),
    "d0": ("sbuf", [128, 1024], "float32"),
    "pp": ("psum", [128, 1024], "float32"), "xx": ("psum", [128, 1024], "float32"), "uu": ("psum", [128, 1024], "float32"),
    "tl": ("psum", [128, 512], "float32"), "hp": ("psum", [128, 512], "float32"),
}
BANKS = [n for n in SCRATCH if SCRATCH[n][0] == "psum"]
DMAS = ["x", "shown", "hist", "sus", "home", "away", "h"] + ["y%d" % u for u in range(U)]
SEMAPHORES = ["q" + q for q in "VSPG"] + ["d_" + n for n in DMAS] + ["arr1", "arr2", "arr3", "sent"]


def routes(T, topo, core):
    peers = [c for c in T.cores if c != core]
    peers = [c for c in peers if topo.die(c) == topo.die(core)] + [c for c in peers if topo.die(c) != topo.die(core)]
    e = topo.engines(core, peers[0])
    return [[(peers[0], e[0::2]), (peers[1], e[1::2])], [(peers[2], topo.engines(core, peers[2]))]]


def part(a, b):
    return b if b < a else b - 1


def build_graph():
    ops, seen = [], {}
    A, F = AluOpType, ActivationFunctionType

    def op(cost, emit, rd=(), wr=(), lat=None, token=None, group=None, deps=()):
        i, dep = len(ops), set(deps)
        acc = [(r, False) for r in rd] + [(r, True) for r in wr]
        acc = [((b, lo // 512 * 512, -(-hi // 512) * 512), True) if b in BANKS else ((b, lo, hi), w) for (b, lo, hi), w in acc]
        for (b, lo, hi), w in acc:
            for l2, h2, j, w2, g2 in seen.get(b, ()):
                if l2 < hi and lo < h2 and (w or w2) and j != i and (group is None or g2 != group):
                    dep.add(j)
        for (b, lo, hi), w in acc:
            old = seen.setdefault(b, [])
            if w and group is None:
                old[:] = [t for t in old if not (lo <= t[0] and t[1] <= hi)]
            old.append((lo, hi, i, w, group))
        ops.append({"cost": cost, "emit": emit, "deps": sorted(dep), "lat": lat, "token": token})
        return i

    def v(n, c=1.0): return {"V": (1, max(64, n * c), 0, 0)}
    def vs(n, c=1.0): return {"V": (1, n * c, 0, 0), "S": (1, n, 0, 0)}
    def gat(n): return {"V": (1, 0, n, 0), "S": (1, 0, n, 0)}
    def pe(k, n): return {"P": (k, 0, 0, k * max(64, n))}
    def gp(n): return {"G": (2, 2 * n, 0, 0)}

    def load(name, dst, lo, hi, q, kb):
        op({q: (1, 0, 0, 0)}, lambda x, q: [x["eng"][q].dma_start(x["T"][dst][:, lo:hi], x["T"][name][:])], wr=[(dst, lo, hi)], lat=("dma", kb), token=name)

    load("shown", "shown_i", 0, 48, "S", 24)
    load("x", "win1", 0, P, "Y", 512)
    load("hist", "c1", 0, 128, "S", 64)
    load("sus", "tab", 0, H, "Y", 1600)
    load("home", "home_i", 0, 512, "S", 800)
    load("away", "away_i", 0, 512, "Y", 2100)

    def fill(buf, rows, lo, hi, val, key=None, step=1):
        op(v((hi - lo) // step), lambda x, q: [x["v"].memset(x["T"][buf][rows[0]:rows[1], lo:hi:step], val)], wr=[(key or buf, 0 if step > 1 else lo, hi)])

    def select(buf, src, rows, lo, hi, slo, shi, pattern, base, cm, rkey, wkey):
        op(gp(hi - lo), lambda x, q: [x["g"].affine_select(x["T"][buf][rows[0]:rows[1], lo:hi], x["T"][src][rows[0]:rows[1], slo:shi], pattern, A.is_equal, 0.0, base, cm)],
           rd=[(rkey, slo, shi)], wr=[(wkey, lo, hi)])

    def iota(buf, rows, n, pattern, base, key):
        op(gp(n), lambda x, q: [x["g"].iota(x["T"][buf][rows[0]:rows[1], 0:n], pattern, base, 0, allow_small_or_imprecise_dtypes=True)], wr=[(key, 0, n)])

    full = (0, 128)
    fill("ones", full, 0, 128, 1.0)
    fill("neg32", full, 0, 128, -32.0)
    select("idn", "ones", full, 0, 128, 0, 128, [[-1, 128]], 0, 1, "ones", "idn")
    select("ri", "ones", full, 0, 128, 0, 128, [[-16, 8], [1, 16]], -15, 1, "ones", "ri")
    select("ris", "neg32", full, 0, 128, 0, 128, [[-16, 8], [1, 16]], -15, 1, "neg32", "ris")
    op(v(128), lambda x, q: [x["v"].tensor_copy(x["T"].rih[:], x["T"].ri[:])], rd=[("ri", 0, 128)], wr=[("rih", 0, 128)])
    fill("d0", full, 0, 1024, 1.0)
    fill("d0", full, 0, 1024, 16777216.0, step=16)
    fill("feat", full, 64, 96 * U, 1.0, step=96, key="one")
    iota("s1f", (64, 96), 16, [[1, 16]], 1, "s1f")
    iota("ev", (0, 32), 512, [[0, 32], [128, 16]], 128, "ev0")
    fill("ev", (32, 64), 0, 512, -64.0, key="ev1")
    op(v(16), lambda x, q: [x["v"].tensor_tensor(x["T"].s1q[64:96, :], x["T"].s1f[64:96, :], x["T"].s1f[64:96, :], A.mult)], rd=[("s1f", 0, 16)], wr=[("s1q", 0, 16)])
    op(v(16), lambda x, q: [x["v"].tensor_scalar(x["T"].em[64:96, 0:16], x["T"].s1q[64:96, :], -64.0, 64.0, A.mult, A.add)], rd=[("s1q", 0, 16)], wr=[("em2", 0, 16)])
    for w in (16, 32, 64, 128, 256):
        op(v(w), lambda x, q, w=w: [x["v"].tensor_copy(x["T"].em[64:96, w:2 * w], x["T"].em[64:96, 0:w])], rd=[("em2", 0, w)], wr=[("em2", w, 2 * w)])
    for f in range(2):
        select("em", "ev", (32 * f, 32 * f + 32), 0, 512, 0, 512, [[-8, 4], [-1, 8], [0, 16]], 0, 1, "ev%d" % f, "em%d" % f)
    EM = [("em0", 0, 512), ("em1", 0, 512), ("em2", 0, 512)]
    select("mz", "ones", (0, 32), 0, 128, 0, 128, [[-1, 8], [0, 4], [-8, 4]], 0, 1, "ones", "mz")
    for h in range(4):
        select("lm", "mz", (0, 32), 128 * h, 128 * h + 128, 0, 128, [[0, 8], [1, 4], [0, 4]], -h, 0, "mz", "lm")

    def copy(dst, src, lo, hi):
        op(v(hi - lo), lambda x, q: [x["v"].tensor_copy(x["T"][dst][:, lo:hi], x["T"][src][:, lo:hi])], rd=[(src, lo, hi)], wr=[(dst, lo, hi)])

    def gather(dst, lo, hi, win, whi, lst, llo, bias, lkey=None):
        k = (hi - lo) // 16

        def emit(x, q):
            T = x["T"]
            a = llo if lkey is None else llo(x)
            o, w = T[dst][:, lo:hi], T[win][:, 0:whi].indirect(T[lst][:, a:a + k])
            if q == "S":
                return [x["s"].activation(o, w, F.Identity, bias=bias)] if bias else [x["s"].activation(o, w, F.Copy)]
            return [x["v"].tensor_scalar(o, w, bias, None, A.add)] if bias else [x["v"].tensor_copy(o, w)]
        lr = (lst, llo, llo + k) if lkey is None else (lst,) + lkey
        return op(gat(hi - lo), emit, rd=[(win, 0, whi), lr], wr=[(dst, lo, hi)])

    def send(d):
        win, snd, arr = "win%d" % d, "snd%d" % d, "arr%d" % d
        for i in range(3):
            def llo(x, i=i):
                to = [t for call in x["routes"] for t in call][i][0]
                return 16 * part(x["rank"], x["T"].rank_of(to))
            gather(snd, S * i, S * i + S, win, P, "shown_u", llo, 0.0, lkey=(0, 48))
        calls, pos = [], 0
        for n, size in enumerate((2, 1)):
            def emit(x, q, n=n, pos=pos):
                T, trs = x["T"], []
                for j, (to, eng) in enumerate(x["routes"][n]):
                    rid, pid, _ = x["topo"].addr(to)
                    at = P + S * part(T.rank_of(to), x["rank"])
                    trs.append((rid, pid, T[win][:, at:at + S], T[snd][:, S * (pos + j):S * (pos + j) + S], sum(1 << e for e in eng)))
                    x["sent"][0] += len(eng)
                if len(trs) == 1:
                    rid, pid, o, a, m = trs[0]
                    x["g"].remote_dma(o, a, T.sem[arr], T.sem["sent"], pid, rid, m)
                else:
                    x["g"].remote_dma_fused([RemoteDMATransfer(dst_ids=[DstId(rid=r, pnc=p)], dma_engine_mask=m, remote_sem=T.sem[arr], srcs=[a], dsts=[o])
                                             for r, p, o, a, m in trs], local_sem=T.sem["sent"])
                return []
            calls.append(op({"G": (12, 0, 0, 0)}, emit, rd=[(snd, S * pos, S * (pos + size))], lat=("remote", 64 * size), token="sent"))
            pos += size
        return op({"-": (0, 0, 0, 0)}, None, wr=[(win, P, W)], token=arr, deps=calls)

    def tables(d, u):
        i0, e, st, b, uu = N * u, N * u + N, "st%d" % (d % 2), N * (u % 2), TWO[u // 2]
        gather("gs", i0, e, "tab", H, "hu%d" % d, i0 // 16, 0.0)
        op(pe(4, 128), lambda x, q: [x["t"].matmul(x["T"][uu][:, b + 128 * k:b + 128 * k + 128], x["T"].gs[:, i0 + k:e:4], x["T"].ris[:], True, True) for k in range(4)],
           rd=[("gs", i0, e), ("ris", 0, 128)], wr=[(uu, b, b + N)])

        def out(x, q):
            o, w = x["T"][st][:, i0:e], x["T"][uu][:, b:b + N]
            return [x["s"].activation(o, w, F.Copy)] if q == "S" else [x["v"].tensor_copy(o, w)]
        op(vs(N), out, rd=[(uu, b, b + N)], wr=[(st, i0, e)])

    def halves(d, u):
        i0, e, dst, win = N * u, N * u + N, "h%d" % d, "win%d" % d
        to = dst if d < DAYS else "hr"
        add = -255.375 if d == 1 else -127.875

        def emit(x, q):
            o, w = x["T"][to][:, i0:e], x["T"][win][:, i0:e]
            return [x["s"].activation(o, w, F.Identity, bias=add, scale=0.5)] if q == "S" else [x["v"].tensor_scalar(o, w, 0.5, add, A.mult, A.add)]
        op(vs(N, 0.5), emit, rd=[(win, i0, e)], wr=[(to, i0, e)])
        if d == DAYS:
            def back(x, q):
                o, w = x["T"][dst][:, i0:e], x["T"].hr[:, i0:e]
                return [x["s"].activation(o, w, F.Identity, bias=255.0)] if q == "S" else [x["v"].tensor_scalar(o, w, 255.0, None, A.add)]
            op(vs(N, 0.5), back, rd=[("hr", i0, e)], wr=[(dst, i0, e)])

    def base(d, u):
        i0, e, hh, uu, b = N * u, N * u + N, "h%d" % d, TWO[u // 2], N * (u % 2)
        op(pe(1, N), lambda x, q: [x["t"].matmul(x["T"][uu][:, b:b + N], x["T"].idn[:], x["T"][hh][:, i0:e], True, False)],
           rd=[(hh, i0, e), ("idn", 0, 128)], wr=[(uu, b, b + N)])

    def low(d):
        c = "c%d" % d
        op(v(128), lambda x, q: [x["v"].tensor_scalar(x["T"].lowc[:], x["T"][c][:], 255, None, A.bitwise_and)], rd=[(c, 0, 128)], wr=[("lowc", 0, 128)])
        op(v(128), lambda x, q: [x["v"].tensor_scalar(x["T"].lowx[:], x["T"].lowc[:], 16.0, -1.0, A.mult, A.add)], rd=[("lowc", 0, 128)], wr=[("lowx", 0, 128)])
        op(v(128, 2), lambda x, q: [x["v"].tensor_tensor(x["T"].ac[:], x["T"].lowx[:], x["T"][c][:], A.subtract)], rd=[("lowx", 0, 128), (c, 0, 128)], wr=[("ac", 0, 128)])

    def pressure(d, u):
        i0, e, b, win, cu = N * u, N * u + N, N * (u % 2), "win%d" % d, "cu%d" % d
        bias = 0.0 if d == 1 else 255.0
        pieces = []
        mine = [c for c in range(4) if (c, u) in PAIRED]
        for c in range(4):
            a = 128 * c + i0 // 16
            if mine and c == 0:
                gather("g0", i0, e, win, W, cu, a, 2 * bias)
                pieces.append(("g2", 0, "rih"))
            elif c in mine:
                op({"V": (1, 0, N, 0)},
                   lambda x, q, a=a: [x["v"].tensor_tensor(x["T"].g2[:, i0:e], x["T"][win][:, 0:W].indirect(x["T"][cu][:, a:a + N // 16]), x["T"].g0[:, i0:e], A.add)],
                   rd=[(win, 0, W), (cu, a, a + N // 16), ("g0", i0, e)], wr=[("g2", i0, e)])
            else:
                gather("gc", P * c + i0, P * c + e, win, W, cu, a, bias)
                pieces.append(("gc", P * c, "ri"))
        last = len(pieces) - 1
        for buf, at, idn in pieces:
            def emit(x, q, buf=buf, at=at + i0, idn=idn):
                T, key = x["T"], (d, u)
                t = x["open"].get(key, 0)
                x["open"][key] = t + 1
                return [x["t"].matmul(T.pp[:, b + 128 * k:b + 128 * k + 128], T[buf][:, at + k:at + N:4], T[idn][:], t == 0 and k == 0, t == last and k == 3) for k in range(4)]
            op(pe(4, 128), emit, rd=[(buf, at + i0, at + e), (idn, 0, 128)], wr=[("pp", b, b + N)], group=(d, u))

    def outcome(d, u0, u1):
        i0, e, n, m0, m1 = N * u0, N * u1, N * (u1 - u0), 32 * u0, 32 * u1
        st, hh, k, uu, b = "st%d" % (d % 2), "h%d" % d, u1 - u0, TWO[u0 // 2], N * (u0 % 2)
        op(v(n), lambda x, q: [x["v"].tensor_tensor(x["T"].sc[:, i0:e], x["T"].pp[:, b:b + n], x["T"][st][:, i0:e], A.mult)], rd=[("pp", b, b + n), (st, i0, e)], wr=[("sc", i0, e)])
        op(v(n), lambda x, q: [x["v"].tensor_tensor_scan(x["T"].fs[:, i0:e], x["T"].d0[:, 0:n], x["T"].sc[:, i0:e], 0.0, A.add, A.min)], rd=[("sc", i0, e), ("d0", 0, 1024)], wr=[("fs", i0, e)])
        op(v(32 * k), lambda x, q: [x["v"].tensor_scalar(x["T"].zi[:, m0:m1], x["T"].fs[:, i0 + 15:e:16], 1.0, -32.0 * TH, A.add, A.min)], rd=[("fs", i0, e)], wr=[("zi", m0, m1)])
        op(v(32 * k), lambda x, q: [x["v"].tensor_scalar(x["T"].zz[:, m0:m1], x["T"].zi[:, m0:m1], 31, None, A.bitwise_and)], rd=[("zi", m0, m1)], wr=[("zz", m0, m1)])
        for u in range(u0, u1):
            a, f, j = 32 * u, 96 * u, 128 * (u - u0)
            op(v(32), lambda x, q, a=a, f=f: [x["v"].tensor_copy(x["T"].feat[:, f:f + 32], x["T"].zz[:, a:a + 32])], rd=[("zz", a, a + 32)], wr=[("feat", f, f + 32)])
            op(v(32, 2), lambda x, q, a=a, f=f: [x["v"].tensor_tensor(x["T"].feat[:, f + 32:f + 64], x["T"].zz[:, a:a + 32], x["T"].zz[:, a:a + 32], A.mult)],
               rd=[("zz", a, a + 32)], wr=[("feat", f + 32, f + 64)])
            op(pe(1, 128), lambda x, q, f=f, j=j: [x["t"].matmul(x["T"].tl[0:65, j:j + 128], x["T"].feat[:, f:f + 65], x["T"].idn[:], True, True)],
               rd=[("feat", f, f + 65), ("one", 0, 96 * U), ("idn", 0, 128)], wr=[("tl", 0, 512)])

        def down(x, q):
            o, w = x["T"].tts[0:65, 128 * u0:128 * u1], x["T"].tl[0:65, 0:128 * k]
            return [x["s"].activation(o, w, F.Copy)] if q == "S" else [x["v"].tensor_copy(o, w)]
        op(vs(128 * k), down, rd=[("tl", 0, 512)], wr=[("tts", 128 * u0, 128 * u1)])
        for u in range(u0, u1):
            j, t = N * (u % 2), 128 * u
            op(pe(4, 128), lambda x, q, j=j, t=t: [x["t"].matmul(x["T"][uu][:, j + r:j + N:4], x["T"].em[0:65, 128 * r:128 * r + 128], x["T"].tts[0:65, t:t + 128], False, r == 3)
                                                   for r in range(4)], rd=[("tts", t, t + 128)] + EM, wr=[(uu, j, j + N)])
        to = "win%d" % (d + 1) if d < DAYS else "yo"
        op(v(n), lambda x, q: [x["v"].tensor_tensor(x["T"][to][:, i0:e], x["T"][uu][:, b:b + n], x["T"][hh][:, i0:e], A.max)], rd=[(uu, b, b + n), (hh, i0, e)], wr=[(to, i0, e)])
        if d == DAYS:
            op({"Y": (1, 0, 0, 0)}, lambda x, q: [x["y"].dma_start(x["T"].y[:, i0:e], x["T"].yo[:, i0:e])], rd=[("yo", i0, e)], lat=("dma", 256 * k), token="y%d" % u0)

    def histories(d, u0, u1):
        lo, hi, k = 32 * u0, 32 * u1, 32 * (u1 - u0)
        z0, h0 = 256, 384
        op(pe(4, k), lambda x, q: [x["t"].matmul(x["T"].tl[:, z0 + lo:z0 + hi], x["T"].lm[0:32, 128 * h:128 * h + 128], x["T"].tts[0:32, 128 * u0 + h:128 * u1:4], h == 0, h == 3)
                                   for h in range(4)], rd=[("tts", 128 * u0, 128 * u1), ("lm", 0, 512)], wr=[("tl", 0, 512)])
        c, cn, hu = "c%d" % d, "c%d" % (d + 1), "hu%d" % (d + 1)
        op(v(k), lambda x, q: [x["v"].tensor_scalar(x["T"].tl[:, h0 + lo:h0 + hi], x["T"].tl[:, z0 + lo:z0 + hi], 1.0, None, A.min)], wr=[("tl", 0, 512)])
        op(v(k), lambda x, q: [x["v"].tensor_tensor(x["T"].t1[:, lo:hi], x["T"].tl[:, h0 + lo:h0 + hi], x["T"].ac[:, lo:hi], A.mult)], rd=[("tl", 0, 512), ("ac", lo, hi)], wr=[("t1", lo, hi)])
        op(v(k), lambda x, q: [x["v"].tensor_tensor(x["T"].t2[:, lo:hi], x["T"].tl[:, z0 + lo:z0 + hi], x["T"].t1[:, lo:hi], A.add)], rd=[("tl", 0, 512), ("t1", lo, hi)], wr=[("t2", lo, hi)])
        op(v(k, 2), lambda x, q: [x["v"].tensor_tensor(x["T"][cn][:, lo:hi], x["T"].t2[:, lo:hi], x["T"][c][:, lo:hi], A.add)], rd=[("t2", lo, hi), (c, lo, hi)], wr=[(cn, lo, hi)])
        if d < DAYS:
            copy(hu, cn, lo, hi)

    def contacts(d):
        for c in range(4):
            lo, hi = 128 * c, 128 * c + 128
            op(v(128), lambda x, q, lo=lo, hi=hi: [x["v"].tensor_tensor(x["T"].hd[:, lo:hi], x["T"].tl[:, 384:512], x["T"].dif[:, lo:hi], A.mult)],
               rd=[("tl", 0, 512), ("dif", lo, hi)], wr=[("hd", lo, hi)])
        op(v(512), lambda x, q: [x["v"].tensor_tensor(x["T"].mg[:], x["T"].hp[:], x["T"].hd[:], A.add)], rd=[("hp", 0, 512), ("hd", 0, 512)], wr=[("mg", 0, 512)])
        copy("cu%d" % d, "mg", 0, 512)

    copy("shown_u", "shown_i", 0, 48)
    send(1)
    copy("hu1", "c1", 0, 128)
    for u in range(U):
        tables(1, u)
    copy("cu1", "home_i", 0, 512)
    copy("hp", "home_i", 0, 512)
    op(v(512), lambda x, q: [x["v"].tensor_tensor(x["T"].dif[:], x["T"].away_i[:], x["T"].hp[:], A.subtract)], rd=[("away_i", 0, 512), ("hp", 0, 512)], wr=[("dif", 0, 512)])
    for d in range(1, DAYS + 1):
        low(d)
        for u in range(U):
            halves(d, u)
        for u in range(U):
            base(d, u)
        for u0, u1 in GROUPS:
            for u in range(u0, u1):
                pressure(d, u)
            outcome(d, u0, u1)
            for b0, b1 in BATCHES:
                if b1 == u1:
                    histories(d, b0, b1)
                    if d < DAYS:
                        for w in range(b0, b1):
                            tables(d + 1, w)
        if d < DAYS:
            send(d + 1)
            contacts(d + 1)
    op({"Y": (1, 0, 0, 0)}, lambda x, q: [x["y"].dma_start(x["T"].h[:], x["T"].c4[:])], rd=[("c4", 0, 128)], lat=("dma", 64), token="h")
    return ops


NOMINAL = {"V": 0.06, "S": 0.10, "P": 0.03, "G": 0.09, "Y": 0.10, "-": 0.0, "cyc": 0.00083, "gat": 1.5 * 0.00083, "pe": 0.00072,
           "hop": 0.10, "own": 0.06, "dma": 2.0, "kb": 0.005, "remote": 2.0, "rkb": 0.008}
SETS = [{}, {"gat": 1.1 * 0.00083, "remote": 2.5}, {"gat": 2.0 * 0.00083}, {"hop": 0.2, "own": 0.1, "pe": 0.00083, "remote": 3.0}]
TRIES = 3000
PLAN = {}


def dur(op, q, m):
    f, cyc, gat, pe = op["cost"][q]
    return f * m[q] + cyc * m["cyc"] + gat * m["gat"] + pe * m["pe"]


def late(op, m):
    if op["lat"] is None:
        return 0.0
    kind, kb = op["lat"]
    return m["dma"] + kb * m["kb"] if kind == "dma" else m["remote"] + kb * m["rkb"]


def schedule(ops, users, m, noise, on):
    n = len(ops)
    prio = [0.0] * n
    for i in range(n - 1, -1, -1):
        prio[i] = dur(ops[i], on[i], m) + late(ops[i], m) + max([prio[j] + m["hop"] for j in users[i]] or [0.0])
    key = [prio[i] + noise[i] for i in range(n)]
    left = [len(o["deps"]) for o in ops]
    done, free = [None] * n, {q: 0.0 for q in "VSPGY-"}
    avail = [i for i in range(n) if left[i] == 0]
    ready, out = [None] * n, []
    while avail:
        best = None
        for i in avail:
            q = on[i]
            if ready[i] is None:
                ready[i] = max([done[d] + (m["own"] if on[d] == q else m["hop"]) for d in ops[i]["deps"]] or [0.0])
            r = max(free[q], ready[i])
            if best is None or r < best[0] - 1e-9 or (r < best[0] + 1e-9 and key[i] > key[best[1]]):
                best = (r, i)
        r, i = best
        q = on[i]
        t = r + dur(ops[i], q, m)
        if q != "-":
            free[q] = t
        done[i] = t + late(ops[i], m)
        out.append((r, i, q))
        avail.remove(i)
        for j in users[i]:
            left[j] -= 1
            if left[j] == 0:
                avail.append(j)
    return out


def replay(ops, order, m):
    done, queue, free, span = {}, {}, {q: 0.0 for q in "VSPGY-"}, 0.0
    for _, i, q in order:
        r = free[q] if q != "-" else 0.0
        for d in ops[i]["deps"]:
            t = done[d] + (m["own"] if queue[d] == q else m["hop"])
            if t > r:
                r = t
        t = r + dur(ops[i], q, m)
        if q != "-":
            free[q] = t
        done[i], queue[i] = t + late(ops[i], m), q
        span = max(span, done[i])
    return span


def plan():
    if PLAN:
        return PLAN
    ops = build_graph()
    n, state = len(ops), [12345]
    users = [[] for _ in range(n)]
    for i, o in enumerate(ops):
        for d in o["deps"]:
            users[d].append(i)

    def rnd(k):
        state[0] = (1103515245 * state[0] + 12345) % 2147483648
        return (state[0] >> 8) % k
    sets = [dict(NOMINAL, **s) for s in SETS]

    def judge(noise, on):
        order = schedule(ops, users, sets[0], noise, on)
        return sum(replay(ops, order, m) for m in sets) / len(sets), order
    flex = [i for i in range(n) if len(ops[i]["cost"]) > 1]
    on = ["S" if len(o["cost"]) > 1 else list(o["cost"])[0] for o in ops]
    noise = [0.0] * n
    best, order = judge(noise, on)
    for _ in range(TRIES):
        noise2, on2 = noise[:], on[:]
        for _ in range(1 << rnd(4)):
            if rnd(5) < 2:
                i = flex[rnd(len(flex))]
                on2[i] = "V" if on[i] == "S" else "S"
            else:
                noise2[rnd(n)] += (rnd(1001) + rnd(1001) + rnd(1001) - 1500) / 250.0
        t, order2 = judge(noise2, on2)
        if t <= best:
            best, order, noise, on = t, order2, noise2, on2
    PLAN["ops"], PLAN["order"], PLAN["time"] = ops, order, best
    PLAN["at"] = {i: k for k, (_, i, _) in enumerate(order)}
    return PLAN


def rank_program(g, core, T, topo):
    rank = T.rank_of(core)
    if rank is None:
        return
    p = plan()
    ops = p["ops"]
    eng = {"V": g.vector, "S": g.scalar, "P": g.tensor, "G": g, "Y": g.sync}
    x = {"g": g, "v": g.vector, "s": g.scalar, "t": g.tensor, "y": g.sync, "T": T, "topo": topo, "rank": rank, "eng": eng,
         "routes": routes(T, topo, core), "open": {}, "sent": [0]}
    landing = sum(len(e) for c in T.cores if c != core for call in routes(T, topo, c) for to, e in call if to == core)
    count = {q: 0 for q in eng}
    seen = {q: {} for q in eng}
    tok, known, final = {}, {}, {}
    for _, i, q in p["order"]:
        o = ops[i]
        if q == "-":
            tok[i], known[i] = (o["token"], landing), {o["token"]: landing}
            final[o["token"]] = landing
            continue
        for d in sorted(o["deps"], key=lambda d: -p["at"][d]):
            s, n = tok[d]
            if n and seen[q].get(s, 0) < n:
                eng[q].wait_ge(T.sem[s], n)
                for s2, n2 in known[d].items():
                    if seen[q].get(s2, 0) < n2:
                        seen[q][s2] = n2
        if q == "G" and o["token"] is None and seen["G"].get("qG", 0) < count["G"]:
            g.wait_ge(T.sem["qG"], count["G"])
            seen["G"]["qG"] = count["G"]
        calls = o["emit"](x, q)
        if o["token"] is None:
            for c in calls:
                count[q] += 1
                c.then_inc(T.sem["q" + q], 1)
            tok[i] = ("q" + q, count[q])
            final["q" + q] = count[q]
        elif o["token"] == "sent":
            tok[i] = ("sent", 0)
        else:
            calls[0].then_inc(T.sem["d_" + o["token"]], 16)
            tok[i] = ("d_" + o["token"], 16)
            final["d_" + o["token"]] = 16
        known[i] = dict(seen[q])
        known[i][tok[i][0]] = max(known[i].get(tok[i][0], 0), tok[i][1])
    final["sent"] = x["sent"][0]
    for s in sorted(final):
        if final[s] and seen["G"].get(s, 0) < final[s]:
            g.wait_ge(T.sem[s], final[s])
